import numpy as np
import ml_dtypes


def mxq(x, axis, fmt="e4m3"):
    dtype, down = {"e4m3": (ml_dtypes.float8_e4m3fn, 7), "e5m2": (ml_dtypes.float8_e5m2, 14)}[fmt]
    v = np.moveaxis(np.asarray(x, np.float32).astype(ml_dtypes.bfloat16).astype(np.float64), axis, -1)
    blocks = v.reshape(v.shape[:-1] + (-1, 32))
    amax = np.abs(blocks).max(-1, keepdims=True)
    byte = np.maximum(np.where(amax > 0, np.frexp(amax)[1] - 1 + 127, 0) - down, 1)
    scale = np.exp2(byte - 127.0)
    codes = (blocks / scale).astype(np.float32).astype(dtype).astype(np.float64)
    return np.moveaxis((codes * scale).reshape(v.shape), -1, axis)


WIDE = False


def mx_kscale(k):
    if not WIDE:
        return np.ones(k)
    levels = np.array([30, -30])
    if k % 512:
        return np.exp2(np.random.permutation(np.resize(levels, k // 32))).repeat(32)
    a = np.empty((k // 512, 16))
    for p in range(k // 512):
        a[p, :8] = np.random.permutation(np.resize(levels, 8))
        for g in range(8):
            far = levels[np.abs(levels - a[p, g]) >= 10]
            a[p, g + 8] = far[np.random.randint(len(far))]
    return np.exp2(a.ravel()).repeat(32)


def f64(x):
    return np.asarray(x).astype(np.float64)


def striped(idx):
    return np.tile(np.asarray(idx).reshape(-1, 16).T, (8, 1)).astype(np.uint16)


def unstriped(offs):
    return offs[:16].T.reshape(-1).astype(np.int64)


E2M1 = np.array([0.0, 0.5, 1.0, 1.5, 2.0, 3.0, 4.0, 6.0, -0.0, -0.5, -1.0, -1.5, -2.0, -3.0, -4.0, -6.0])


def pack_weight(w, fmt):
    k, n = w.shape
    w = f64(np.asarray(w, np.float32).astype(ml_dtypes.bfloat16)).reshape(k // 32, 32, n)
    amax = np.abs(w).max(1)
    if fmt in ("e4m3", "e5m2"):
        byte = np.frexp(amax)[1] - 1 + 127 - (7 if fmt == "e4m3" else 14)
    else:
        mant, ex = np.frexp(amax / 6.0)
        byte = np.where(mant > 0.5, ex, ex - 1) + 127
    byte = np.clip(np.where(amax > 0, byte, 1), 1, 254)
    scaled = (w * np.exp2(127.0 - byte)[:, None, :]).reshape(k, n).astype(np.float32)
    by_word = np.ascontiguousarray(scaled.reshape(k // 512, 128, 4, n).transpose(0, 1, 3, 2))
    if fmt in ("e4m3", "e5m2"):
        words = by_word.astype(ml_dtypes.float8_e4m3fn if fmt == "e4m3" else ml_dtypes.float8_e5m2).view(np.uint8)
    else:
        c = by_word.astype(ml_dtypes.float4_e2m1fn).view(np.uint8) & 0xF
        words = (c[..., 0::2] | (c[..., 1::2] << 4)).reshape(k // 512, 128, 2 * n)
    return np.ascontiguousarray(words), np.ascontiguousarray(byte.astype(np.uint8).reshape(k // 512, 16, n))


def unpack_weight(words, scales, fmt):
    g, _, n = scales.shape
    words = np.ascontiguousarray(words).reshape(g, 128, n, -1)
    if fmt in ("e4m3", "e5m2"):
        vals = words.view(ml_dtypes.float8_e4m3fn if fmt == "e4m3" else ml_dtypes.float8_e5m2).astype(np.float64)
    else:
        nib = np.empty((g, 128, n, 4), np.uint8)
        nib[..., 0::2] = words & 0xF
        nib[..., 1::2] = words >> 4
        vals = E2M1[nib]
    vals = vals * np.repeat(np.exp2(scales.astype(np.float64) - 127.0), 8, axis=1)[..., None]
    return vals.transpose(0, 1, 3, 2).reshape(g * 512, n)


K, T, J, R, C, O, N, S, E = 512, 1024, 256, 512, 512, 128, 256, 1024, 512


def setup_inputs():
    n = np.random.standard_normal
    idx = np.random.permutation(T)[:J]
    idx2 = np.random.permutation(C)[:J]
    idx3 = np.random.permutation(C)[:O]
    idx4 = np.random.permutation(J)[:O]
    idx5 = np.random.permutation(S)[:N]
    idx6 = np.random.permutation(E)[:O]
    idx7 = np.random.permutation(E)[:O]
    fk = mx_kscale(K)
    fr = mx_kscale(R)
    xtp = pack_weight(n((K, T)) / fk[:, None], "e5m2")
    wp = pack_weight(n((K, R)) * 1 / np.sqrt(K) * fk[:, None] * fr, "e2m1")
    w2p = pack_weight(n((K, R)) * 1 / np.sqrt(K) * fk[:, None], "e4m3")
    vsp = pack_weight(n((R, S)) * 1 / np.sqrt(R) / fr[:, None], "e2m1")
    return {
        "xt_words": xtp[0],
        "xt_scales": xtp[1],
        "w_words": wp[0],
        "w_scales": wp[1],
        "w2_words": w2p[0],
        "w2_scales": w2p[1],
        "vs_words": vsp[0],
        "vs_scales": vsp[1],
        "offs": striped(idx),
        "offs2": striped(idx2),
        "offs3": striped(idx3),
        "offs4": striped(idx4),
        "offs5": striped(idx5),
        "offs6": striped(idx6),
        "offs7": striped(idx7),
    }


def reference(xt_words, xt_scales, w_words, w_scales, w2_words, w2_scales, vs_words, vs_scales, offs, offs2, offs3, offs4, offs5, offs6, offs7):
    idx = unstriped(offs)
    idx2 = unstriped(offs2)
    idx3 = unstriped(offs3)
    idx4 = unstriped(offs4)
    idx5 = unstriped(offs5)
    idx6 = unstriped(offs6)
    idx7 = unstriped(offs7)
    xtu = unpack_weight(xt_words, xt_scales, "e5m2")
    wu = unpack_weight(w_words, w_scales, "e2m1")
    w2u = unpack_weight(w2_words, w2_scales, "e4m3")
    vsu = unpack_weight(vs_words, vs_scales, "e2m1")
    xtidxg = xtu[:, idx]
    a = wu.T @ xtidxg
    b = w2u.T @ xtidxg
    lb = b[:, 0:1]
    la = a[:, 0:1]
    pw = np.zeros((R, C))
    pw[:, idx2] = a
    hid = np.maximum(pw[:, idx3] * lb, b[:, idx4] * la)
    vsidx5g = vsu[:, idx5]
    hidq = mxq(hid, 0, "e4m3")
    p = vsidx5g.T @ hidq
    pa = np.zeros((N, E))
    pa[:, idx6] = p
    pb = np.zeros((N, E))
    pb[:, idx7] = p
    y = pa + pb
    return y

@@ -1,0 +1,198 @@
+from contextlib import ExitStack
+
+import concourse.mybir as mybir
+
+K, T, J, R, C, O, N, S, E = 512, 1024, 256, 512, 512, 128, 256, 1024, 512
+FLOPS = 2 * (2 * K * R * J + R * N * O)
+
+F32 = mybir.dt.float32
+BF16 = mybir.dt.bfloat16
+I32 = mybir.dt.int32
+U32 = mybir.dt.uint32
+U16 = mybir.dt.uint16
+U8 = mybir.dt.uint8
+E4M3 = mybir.dt.float8_e4m3fn_x4
+E5M2 = mybir.dt.float8_e5m2_x4
+E2M1 = mybir.dt.float4_e2m1fn_x4
+COPY = mybir.ActivationFunctionType.Copy
+ADD = mybir.AluOpType.add
+MAX = mybir.AluOpType.max
+
+P = 128
+PACK = 4
+QUADS = 4
+QUAD = 32
+
+
+def tile_list_leadboard_twow_store_pagetwice_kernel(
+    tc, xt_words, xt_scales, w_words, w_scales, w2_words, w2_scales, vs_words, vs_scales,
+    offs, offs2, offs3, offs4, offs5, offs6, offs7, out,
+):
+    nc = tc.nc
+    with ExitStack() as ctx:
+        lists = ctx.enter_context(tc.tile_pool(name="lists", bufs=1))
+        sb = ctx.enter_context(tc.tile_pool(name="sb", bufs=1))
+        psum = ctx.enter_context(tc.psum_pool(name="psum", bufs=1))
+
+        def load_list(src, name):
+            t = lists.tile(list(src.shape), U16, name=name)
+            nc.sync.dma_start(t[:], src)
+            return t
+
+        def zero_plane(width, name, tag):
+            t = sb.tile([P, width], U8, name=name, tag=tag, align_bytes=64)
+            nc.vector.memset(t[:].bitcast(I32), 0)
+            return t
+
+        def load_plane(plane, src):
+            for q in range(QUADS):
+                nc.sync.dma_start(
+                    plane[QUAD * q : QUAD * q + PACK, :].bitcast(I32),
+                    src[0, PACK * q : PACK * (q + 1), :].bitcast(I32),
+                )
+
+        def deal(engine_copy, src, dtype, name, tag=None):
+            t = sb.tile([P, R], dtype, name=name, tag=tag or name, align_bytes=64)
+            engine_copy(
+                out=t[:].rearrange("p (t m) -> p m t", t=PACK),
+                in_=src[:, 0:R].rearrange("p (m t) -> p m t", t=PACK),
+            )
+            return t
+
+        def gpsimd_deal(out, in_):
+            nc.gpsimd.tensor_copy(out=out.rearrange("p m t -> p t m"), in_=in_.rearrange("p m t -> p t m"))
+
+        def gather(window, offsets, width, dtype, name, tag=None):
+            t = sb.tile([P, width], dtype, name=name, tag=tag or name, align_bytes=64)
+            nc.vector.tensor_copy(out=t[:], in_=window[:].indirect(offsets[:]))
+            return t
+
+        ws_plane = zero_plane(2 * R, "ws_plane", "ws_plane")
+        xs_plane = zero_plane(T, "xs_plane", "xs_plane")
+        w2s_plane = zero_plane(R, "w2s_plane", "page0")
+        vs_plane = zero_plane(S, "vs_plane", "vs_plane")
+
+        boards = []
+        for t in range(PACK):
+            board = sb.tile([P, C], F32, name="board%d" % t)
+            nc.gpsimd.memset(board[:], 0.0)
+            boards.append(board)
+
+        l_tok = load_list(offs, "l_tok")
+        x_all = sb.tile([P, T], U32, name="x_all", align_bytes=64)
+        nc.sync.dma_start(x_all[:].bitcast(I32), xt_words[0].rearrange("p n t -> p (n t)").bitcast(I32))
+        ws_rows = w_scales[0].rearrange("(h q r) c -> q r h c", h=2, r=PACK).bitcast(I32)
+        for q in range(2):
+            nc.sync.dma_start(
+                ws_plane[QUAD * q : QUAD * q + PACK, :].bitcast(I32).rearrange("p (h c) -> p h c", h=2),
+                ws_rows[q],
+            )
+        load_plane(xs_plane, xt_scales)
+        w_raw = sb.tile([P, R], U16, name="w_raw", align_bytes=64)
+        nc.sync.dma_start(w_raw[:].bitcast(I32), w_words[0].bitcast(I32))
+        l_board = load_list(offs2, "l_board")
+        w2_raw = sb.tile([P, R], U32, name="w2_raw", align_bytes=64)
+        nc.sync.dma_start(w2_raw[:].bitcast(I32), w2_words[0].rearrange("p n t -> p (n t)").bitcast(I32))
+        load_plane(w2s_plane, w2_scales)
+        l_slot = load_list(offs4, "l_slot")
+        l_pick = load_list(offs3, "l_pick")
+        v_all = sb.tile([P, S], U16, name="v_all", align_bytes=64)
+        nc.sync.dma_start(v_all[:].bitcast(I32), vs_words[0].bitcast(I32))
+        l_store = load_list(offs5, "l_store")
+        load_plane(vs_plane, vs_scales)
+        l_pages = [load_list(offs6, "l_page_a"), load_list(offs7, "l_page_b")]
+
+        nc.vector.tensor_copy(
+            out=ws_plane[P // 2 :, 0:R].bitcast(I32), in_=ws_plane[: P // 2, R : 2 * R].bitcast(I32)
+        )
+        w_scale = deal(nc.vector.tensor_copy, ws_plane, U8, "w_scale")
+        w_code = deal(nc.scalar.copy, w_raw, U16, "w_code")
+        x_scale = gather(xs_plane, l_tok, J, U8, "x_scale")
+        x_code = gather(x_all, l_tok, J, U32, "x_code", "page3")
+        w2_code = deal(nc.scalar.copy, w2_raw, U32, "w2_code", "page1")
+
+        def stage_one(code, scale, fmt, t, tag):
+            acc = psum.tile([P, J], F32, name="acc", tag=tag)
+            cols = slice(P * t, P * (t + 1))
+            nc.tensor.matmul_mx(
+                out=acc[:], lhsT=code[:, cols].bitcast(fmt), lhsT_scale=scale[:, cols],
+                rhs=x_code[:].bitcast(E5M2), rhs_scale=x_scale[:], start=True, stop=True,
+            )
+            return acc
+
+        def to_sbuf(engine_copy, acc, width, name):
+            t = sb.tile([P, width], F32, name=name, tag=name, align_bytes=64)
+            engine_copy(out=t[:], in_=acc[:])
+            return t
+
+        def scatter_vector(window, offsets, values):
+            nc.vector.tensor_copy(out=window[:].indirect(offsets[:]), in_=values[:])
+
+        def scatter_scalar(window, offsets, values):
+            nc.scalar.activation(out=window[:].indirect(offsets[:]), in_=values[:], func=COPY)
+
+        a_acc = {t: stage_one(w_code, w_scale, E2M1, t, "a_acc%d" % t) for t in (0, 1, 3)}
+        a = [None] * PACK
+        a[0] = to_sbuf(nc.vector.tensor_copy, a_acc[0], J, "a0")
+        a[1] = to_sbuf(nc.scalar.copy, a_acc[1], J, "a1")
+        scatter_vector(boards[0], l_board, a[0])
+        scatter_scalar(boards[1], l_board, a[1])
+        a[3] = to_sbuf(nc.scalar.copy, a_acc[3], J, "a3")
+        scatter_scalar(boards[3], l_board, a[3])
+        w2_scale = deal(gpsimd_deal, w2s_plane, U8, "w2_scale", "page2")
+        v_scale = gather(vs_plane, l_store, N, U8, "v_scale")
+        b_acc = [stage_one(w2_code, w2_scale, E4M3, t, "b_acc%d" % t) for t in range(PACK)]
+        b = [to_sbuf(nc.vector.tensor_copy, b_acc[t], J, "b%d" % t) for t in range(PACK)]
+        a_acc[2] = stage_one(w_code, w_scale, E2M1, 2, "b_acc1")
+        a[2] = to_sbuf(nc.vector.tensor_copy, a_acc[2], J, "a2")
+        scatter_vector(boards[2], l_board, a[2])
+
+        pages = []
+        for i in range(4):
+            page = sb.tile([P, E], F32, name="page%d" % i, tag="page%d" % i, align_bytes=64)
+            nc.gpsimd.memset(page[:], 0.0)
+            pages.append(page)
+
+        from_board = sb.tile([P, PACK, O], F32, name="from_board")
+        from_slot = sb.tile([P, PACK, O], F32, name="from_slot")
+        for t in (0, 1, 3, 2):
+            nc.scalar.activation(
+                out=from_slot[:, t, :], in_=b[t][:].indirect(l_slot[:]), func=COPY, scale=a[t][:, 0:1]
+            )
+            nc.scalar.activation(
+                out=from_board[:, t, :], in_=boards[t][:].indirect(l_pick[:]), func=COPY, scale=b[t][:, 0:1]
+            )
+
+        v_code = gather(v_all, l_store, N, U16, "v_code", "a2")
+
+        hid = sb.tile([P, O * PACK], BF16, name="hid", align_bytes=64)
+        nc.vector.tensor_tensor(
+            out=hid[:].rearrange("p (c i t) -> p c t i", i=4, t=PACK),
+            in0=from_board[:].rearrange("p t (c i) -> p c t i", i=4),
+            in1=from_slot[:].rearrange("p t (c i) -> p c t i", i=4),
+            op=MAX,
+        )
+        h_code = sb.tile([P, O], U32, name="h_code", align_bytes=64)
+        h_scale = sb.tile([P, O], U8, name="h_scale", align_bytes=64)
+        nc.vector.quantize_mx(out=h_code[:].bitcast(E4M3), scales=h_scale[:], in_=hid[:])
+
+        halves = N // P
+        p_acc = []
+        for h in range(halves):
+            acc = psum.tile([P, O], F32, name="p_acc%d" % h, tag="a_acc%d" % h)
+            cols = slice(P * h, P * (h + 1))
+            nc.tensor.matmul_mx(
+                out=acc[:], lhsT=v_code[:, cols].bitcast(E2M1), lhsT_scale=v_scale[:, cols],
+                rhs=h_code[:].bitcast(E4M3), rhs_scale=h_scale[:], start=True, stop=True,
+            )
+            p_acc.append(acc)
+        p = [
+            to_sbuf(nc.vector.tensor_copy, p_acc[0], O, "p0"),
+            to_sbuf(nc.scalar.copy, p_acc[1], O, "p1"),
+        ]
+        for h in range(halves):
+            scatter_vector(pages[2 * h], l_pages[0], p[h])
+            scatter_scalar(pages[2 * h + 1], l_pages[1], p[h])
+            y = sb.tile([P, E], F32, name="y%d" % h)
+            nc.vector.tensor_tensor(out=y[:], in0=pages[2 * h][:], in1=pages[2 * h + 1][:], op=ADD)
+            nc.sync.dma_start(out[P * h : P * (h + 1), :], y[:])

@@ -22,6 +22,7 @@ P = 128
 PACK = 4
 QUADS = 4
 QUAD = 32
+SPLIT = 320
 
 
 def tile_list_leadboard_twow_store_pagetwice_kernel(
@@ -59,63 +60,66 @@ def tile_list_leadboard_twow_store_pagetwice_kernel(
             )
             return t
 
-        def gpsimd_deal(out, in_):
-            nc.gpsimd.tensor_copy(out=out.rearrange("p m t -> p t m"), in_=in_.rearrange("p m t -> p t m"))
+        def deal_slice(engine_copy, src, dtype, t, name):
+            dealt = sb.tile([P, P], dtype, name=name, tag=name, align_bytes=64)
+            engine_copy(out=dealt[:], in_=src[:].rearrange("p (m t) -> p t m", t=PACK)[:, t, :])
+            return dealt
+
+        def deal_scales(plane, t, name):
+            return deal_slice(nc.gpsimd.tensor_copy, plane, U8, t, name)
 
         def gather(window, offsets, width, dtype, name, tag=None):
             t = sb.tile([P, width], dtype, name=name, tag=tag or name, align_bytes=64)
             nc.vector.tensor_copy(out=t[:], in_=window[:].indirect(offsets[:]))
             return t
 
-        ws_plane = zero_plane(2 * R, "ws_plane", "ws_plane")
         xs_plane = zero_plane(T, "xs_plane", "xs_plane")
-        w2s_plane = zero_plane(R, "w2s_plane", "page0")
+        ws_plane = zero_plane(R, "ws_plane", "ws_plane")
+        w2s_plane = zero_plane(R, "w2s_plane", "w2s_plane")
         vs_plane = zero_plane(S, "vs_plane", "vs_plane")
 
-        boards = []
-        for t in range(PACK):
-            board = sb.tile([P, C], F32, name="board%d" % t)
-            nc.gpsimd.memset(board[:], 0.0)
-            boards.append(board)
+        def zeroed(engine, width, name, tag):
+            t = sb.tile([P, width], F32, name=name, tag=tag, align_bytes=64)
+            engine.memset(t[:], 0.0)
+            return t
 
-        l_tok = load_list(offs, "l_tok")
+        boards = {t: zeroed(nc.vector, C, "board%d" % t, "board%d" % t) for t in (1, 0, 3)}
+
+        ws_rows = sb.tile([PACK, QUADS, R // 4], I32, name="ws_rows")
+        nc.sync.dma_start(ws_rows[:], w_scales[0].rearrange("(q r) c -> r q c", r=PACK).bitcast(I32))
         x_all = sb.tile([P, T], U32, name="x_all", align_bytes=64)
-        nc.sync.dma_start(x_all[:].bitcast(I32), xt_words[0].rearrange("p n t -> p (n t)").bitcast(I32))
-        ws_rows = w_scales[0].rearrange("(h q r) c -> q r h c", h=2, r=PACK).bitcast(I32)
-        for q in range(2):
-            nc.sync.dma_start(
-                ws_plane[QUAD * q : QUAD * q + PACK, :].bitcast(I32).rearrange("p (h c) -> p h c", h=2),
-                ws_rows[q],
-            )
+        nc.scalar.dma_start(x_all[:].bitcast(I32), xt_words[0].rearrange("p n t -> p (n t)").bitcast(I32))
+        l_tok = load_list(offs, "l_tok")
         load_plane(xs_plane, xt_scales)
         w_raw = sb.tile([P, R], U16, name="w_raw", align_bytes=64)
         nc.sync.dma_start(w_raw[:].bitcast(I32), w_words[0].bitcast(I32))
-        l_board = load_list(offs2, "l_board")
         w2_raw = sb.tile([P, R], U32, name="w2_raw", align_bytes=64)
         nc.sync.dma_start(w2_raw[:].bitcast(I32), w2_words[0].rearrange("p n t -> p (n t)").bitcast(I32))
+        l_board = load_list(offs2, "l_board")
         load_plane(w2s_plane, w2_scales)
         l_slot = load_list(offs4, "l_slot")
         l_pick = load_list(offs3, "l_pick")
-        v_all = sb.tile([P, S], U16, name="v_all", align_bytes=64)
+        v_all = sb.tile([P, S], U16, name="v_all", tag="v_all", align_bytes=64)
         nc.sync.dma_start(v_all[:].bitcast(I32), vs_words[0].bitcast(I32))
         l_store = load_list(offs5, "l_store")
         load_plane(vs_plane, vs_scales)
         l_pages = [load_list(offs6, "l_page_a"), load_list(offs7, "l_page_b")]
 
-        nc.vector.tensor_copy(
-            out=ws_plane[P // 2 :, 0:R].bitcast(I32), in_=ws_plane[: P // 2, R : 2 * R].bitcast(I32)
-        )
-        w_scale = deal(nc.vector.tensor_copy, ws_plane, U8, "w_scale")
-        w_code = deal(nc.scalar.copy, w_raw, U16, "w_code")
+        for q in range(QUADS):
+            nc.vector.tensor_copy(
+                out=ws_plane[QUAD * q : QUAD * q + PACK, :].bitcast(I32), in_=ws_rows[:, q, :]
+            )
+        w_scale = {t: deal_scales(ws_plane, t, "w_scale%d" % t) for t in (1, 0, 3, 2)}
+        w_code = {t: deal_slice(nc.scalar.copy, w_raw, U16, t, "w_code%d" % t)[:] for t in (1, 0, 3, 2)}
         x_scale = gather(xs_plane, l_tok, J, U8, "x_scale")
-        x_code = gather(x_all, l_tok, J, U32, "x_code", "page3")
-        w2_code = deal(nc.scalar.copy, w2_raw, U32, "w2_code", "page1")
+        x_code = gather(x_all, l_tok, J, U32, "x_code")
+        w2_dealt = deal(nc.vector.tensor_copy, w2_raw, U32, "w2_code")
+        w2_code = [w2_dealt[:, P * t : P * (t + 1)] for t in range(PACK)]
 
         def stage_one(code, scale, fmt, t, tag):
             acc = psum.tile([P, J], F32, name="acc", tag=tag)
-            cols = slice(P * t, P * (t + 1))
             nc.tensor.matmul_mx(
-                out=acc[:], lhsT=code[:, cols].bitcast(fmt), lhsT_scale=scale[:, cols],
+                out=acc[:], lhsT=code[t].bitcast(fmt), lhsT_scale=scale[t][:],
                 rhs=x_code[:].bitcast(E5M2), rhs_scale=x_scale[:], start=True, stop=True,
             )
             return acc
@@ -131,50 +135,56 @@ def tile_list_leadboard_twow_store_pagetwice_kernel(
         def scatter_scalar(window, offsets, values):
             nc.scalar.activation(out=window[:].indirect(offsets[:]), in_=values[:], func=COPY)
 
-        a_acc = {t: stage_one(w_code, w_scale, E2M1, t, "a_acc%d" % t) for t in (0, 1, 3)}
+        a_acc = {t: stage_one(w_code, w_scale, E2M1, t, "a_acc%d" % t) for t in (1, 0, 3, 2)}
         a = [None] * PACK
-        a[0] = to_sbuf(nc.vector.tensor_copy, a_acc[0], J, "a0")
         a[1] = to_sbuf(nc.scalar.copy, a_acc[1], J, "a1")
+        a[0] = to_sbuf(nc.vector.tensor_copy, a_acc[0], J, "a0")
+        a[3] = to_sbuf(nc.vector.tensor_copy, a_acc[3], J, "a3")
+        a[2] = to_sbuf(nc.vector.tensor_copy, a_acc[2], J, "a2")
         scatter_vector(boards[0], l_board, a[0])
         scatter_scalar(boards[1], l_board, a[1])
-        a[3] = to_sbuf(nc.scalar.copy, a_acc[3], J, "a3")
         scatter_scalar(boards[3], l_board, a[3])
-        w2_scale = deal(gpsimd_deal, w2s_plane, U8, "w2_scale", "page2")
-        v_scale = gather(vs_plane, l_store, N, U8, "v_scale")
+        w2_scale = [deal_scales(w2s_plane, t, "w2_scale%d" % t) for t in range(PACK)]
         b_acc = [stage_one(w2_code, w2_scale, E4M3, t, "b_acc%d" % t) for t in range(PACK)]
         b = [to_sbuf(nc.vector.tensor_copy, b_acc[t], J, "b%d" % t) for t in range(PACK)]
-        a_acc[2] = stage_one(w_code, w_scale, E2M1, 2, "b_acc1")
-        a[2] = to_sbuf(nc.vector.tensor_copy, a_acc[2], J, "a2")
+        boards[2] = zeroed(nc.gpsimd, C, "board2", "w2_scale3")
         scatter_vector(boards[2], l_board, a[2])
-
-        pages = []
-        for i in range(4):
-            page = sb.tile([P, E], F32, name="page%d" % i, tag="page%d" % i, align_bytes=64)
-            nc.gpsimd.memset(page[:], 0.0)
-            pages.append(page)
 
         from_board = sb.tile([P, PACK, O], F32, name="from_board")
         from_slot = sb.tile([P, PACK, O], F32, name="from_slot")
-        for t in (0, 1, 3, 2):
+        for t in range(PACK):
             nc.scalar.activation(
                 out=from_slot[:, t, :], in_=b[t][:].indirect(l_slot[:]), func=COPY, scale=a[t][:, 0:1]
             )
+        for t in (0, 1, 3, 2):
             nc.scalar.activation(
                 out=from_board[:, t, :], in_=boards[t][:].indirect(l_pick[:]), func=COPY, scale=b[t][:, 0:1]
             )
 
-        v_code = gather(v_all, l_store, N, U16, "v_code", "a2")
+        pages = [zeroed(nc.gpsimd, E, "page%d" % i, "a%d" % t) for i, t in enumerate((0, 1, 3, 2))]
 
-        hid = sb.tile([P, O * PACK], BF16, name="hid", align_bytes=64)
-        nc.vector.tensor_tensor(
-            out=hid[:].rearrange("p (c i t) -> p c t i", i=4, t=PACK),
-            in0=from_board[:].rearrange("p t (c i) -> p c t i", i=4),
-            in1=from_slot[:].rearrange("p t (c i) -> p c t i", i=4),
-            op=MAX,
-        )
+        v_scale = gather(vs_plane, l_store, N, U8, "v_scale")
+        v_code = gather(v_all, l_store, N, U16, "v_code", "vs_plane")
+
+        hid = [
+            sb.tile([P, O // 2, PACK], BF16, name="hid%d" % i, tag=tag, align_bytes=64)
+            for i, tag in enumerate(("v_all", "hid1"))
+        ]
         h_code = sb.tile([P, O], U32, name="h_code", align_bytes=64)
         h_scale = sb.tile([P, O], U8, name="h_scale", align_bytes=64)
-        nc.vector.quantize_mx(out=h_code[:].bitcast(E4M3), scales=h_scale[:], in_=hid[:])
+        parts = [slice(0, O // 2), slice(O // 2, O)]
+        for half, cols in zip(hid, parts):
+            nc.vector.tensor_tensor(
+                out=half[:].rearrange("p (c i) t -> p c t i", i=4),
+                in0=from_board[:, :, cols].rearrange("p t (c i) -> p c t i", i=4),
+                in1=from_slot[:, :, cols].rearrange("p t (c i) -> p c t i", i=4),
+                op=MAX,
+            )
+        for half, cols in zip(hid, parts):
+            nc.vector.quantize_mx(
+                out=h_code[:, cols].bitcast(E4M3), scales=h_scale[:, cols],
+                in_=half[:].rearrange("p o t -> p (o t)"),
+            )
 
         halves = N // P
         p_acc = []
@@ -193,6 +203,18 @@ def tile_list_leadboard_twow_store_pagetwice_kernel(
         for h in range(halves):
             scatter_vector(pages[2 * h], l_pages[0], p[h])
             scatter_scalar(pages[2 * h + 1], l_pages[1], p[h])
-            y = sb.tile([P, E], F32, name="y%d" % h)
-            nc.vector.tensor_tensor(out=y[:], in0=pages[2 * h][:], in1=pages[2 * h + 1][:], op=ADD)
-            nc.sync.dma_start(out[P * h : P * (h + 1), :], y[:])
+
+        def add_pages(engine, y, h, cols):
+            engine.tensor_tensor(
+                out=y[:, cols], in0=pages[2 * h][:, cols], in1=pages[2 * h + 1][:, cols], op=ADD
+            )
+
+        y0 = sb.tile([P, E], F32, name="y0")
+        add_pages(nc.gpsimd, y0, 0, slice(0, SPLIT))
+        nc.sync.dma_start(out[0:P, 0:SPLIT], y0[:, 0:SPLIT])
+        add_pages(nc.vector, y0, 0, slice(SPLIT, E))
+        nc.sync.dma_start(out[0:P, SPLIT:E], y0[:, SPLIT:E])
+        y1 = sb.tile([P, E], F32, name="y1")
+        for cols in (slice(0, E // 2), slice(E // 2, E)):
+            add_pages(nc.vector, y1, 1, cols)
+            nc.sync.dma_start(out[P : 2 * P, cols], y1[:, cols])

@@ -22,7 +22,7 @@ P = 128
 PACK = 4
 QUADS = 4
 QUAD = 32
-SPLIT = 320
+SPLIT = 256
 
 
 def tile_list_leadboard_twow_store_pagetwice_kernel(
@@ -111,16 +111,21 @@ def tile_list_leadboard_twow_store_pagetwice_kernel(
             )
         w_scale = {t: deal_scales(ws_plane, t, "w_scale%d" % t) for t in (1, 0, 3, 2)}
         w_code = {t: deal_slice(nc.scalar.copy, w_raw, U16, t, "w_code%d" % t)[:] for t in (1, 0, 3, 2)}
-        x_scale = gather(xs_plane, l_tok, J, U8, "x_scale")
-        x_code = gather(x_all, l_tok, J, U32, "x_code")
+        x_scale = sb.tile([P, J], U8, name="x_scale", align_bytes=64)
+        x_code = sb.tile([P, J], U32, name="x_code", align_bytes=64)
+        slots = [slice(0, J // 2), slice(J // 2, J)]
+        entries = [slice(0, J // 32), slice(J // 32, J // 16)]
+        for cols, ents in zip(slots, entries):
+            nc.vector.tensor_copy(out=x_scale[:, cols], in_=xs_plane[:].indirect(l_tok[:, ents]))
+            nc.vector.tensor_copy(out=x_code[:, cols], in_=x_all[:].indirect(l_tok[:, ents]))
         w2_dealt = deal(nc.vector.tensor_copy, w2_raw, U32, "w2_code")
         w2_code = [w2_dealt[:, P * t : P * (t + 1)] for t in range(PACK)]
 
-        def stage_one(code, scale, fmt, t, tag):
-            acc = psum.tile([P, J], F32, name="acc", tag=tag)
+        def stage_one(code, scale, fmt, t, tag, cols=slice(0, J)):
+            acc = psum.tile([P, cols.stop - cols.start], F32, name="acc", tag=tag)
             nc.tensor.matmul_mx(
                 out=acc[:], lhsT=code[t].bitcast(fmt), lhsT_scale=scale[t][:],
-                rhs=x_code[:].bitcast(E5M2), rhs_scale=x_scale[:], start=True, stop=True,
+                rhs=x_code[:, cols].bitcast(E5M2), rhs_scale=x_scale[:, cols], start=True, stop=True,
             )
             return acc
 
@@ -135,14 +140,25 @@ def tile_list_leadboard_twow_store_pagetwice_kernel(
         def scatter_scalar(window, offsets, values):
             nc.scalar.activation(out=window[:].indirect(offsets[:]), in_=values[:], func=COPY)
 
-        a_acc = {t: stage_one(w_code, w_scale, E2M1, t, "a_acc%d" % t) for t in (1, 0, 3, 2)}
-        a = [None] * PACK
-        a[1] = to_sbuf(nc.scalar.copy, a_acc[1], J, "a1")
-        a[0] = to_sbuf(nc.vector.tensor_copy, a_acc[0], J, "a0")
-        a[3] = to_sbuf(nc.vector.tensor_copy, a_acc[3], J, "a3")
-        a[2] = to_sbuf(nc.vector.tensor_copy, a_acc[2], J, "a2")
+        a = [sb.tile([P, J], F32, name="a%d" % t, tag="a%d" % t, align_bytes=64) for t in range(PACK)]
+        lo, hi = slots
+        acc = stage_one(w_code, w_scale, E2M1, 1, "a_acc1", lo)
+        nc.scalar.copy(out=a[1][:, lo], in_=acc[:])
+        nc.scalar.activation(
+            out=boards[1][:].indirect(l_board[:, entries[0]]), in_=a[1][:, lo], func=COPY
+        )
+        acc = stage_one(w_code, w_scale, E2M1, 0, "a_acc0")
+        nc.vector.tensor_copy(out=a[0][:], in_=acc[:])
+        acc = stage_one(w_code, w_scale, E2M1, 1, "a_acc1", hi)
+        nc.vector.tensor_copy(out=a[1][:, hi], in_=acc[:])
+        acc = stage_one(w_code, w_scale, E2M1, 3, "a_acc3")
+        nc.vector.tensor_copy(out=a[3][:], in_=acc[:])
+        nc.scalar.activation(
+            out=boards[1][:].indirect(l_board[:, entries[1]]), in_=a[1][:, hi], func=COPY
+        )
         scatter_vector(boards[0], l_board, a[0])
-        scatter_scalar(boards[1], l_board, a[1])
+        acc = stage_one(w_code, w_scale, E2M1, 2, "a_acc2")
+        nc.scalar.copy(out=a[2][:], in_=acc[:])
         scatter_scalar(boards[3], l_board, a[3])
         w2_scale = [deal_scales(w2s_plane, t, "w2_scale%d" % t) for t in range(PACK)]
         b_acc = [stage_one(w2_code, w2_scale, E4M3, t, "b_acc%d" % t) for t in range(PACK)]
@@ -166,24 +182,21 @@ def tile_list_leadboard_twow_store_pagetwice_kernel(
         v_scale = gather(vs_plane, l_store, N, U8, "v_scale")
         v_code = gather(v_all, l_store, N, U16, "v_code", "vs_plane")
 
-        hid = [
-            sb.tile([P, O // 2, PACK], BF16, name="hid%d" % i, tag=tag, align_bytes=64)
-            for i, tag in enumerate(("v_all", "hid1"))
-        ]
+        hid = sb.tile([P, O, PACK], BF16, name="hid", tag="v_all", align_bytes=64)
         h_code = sb.tile([P, O], U32, name="h_code", align_bytes=64)
         h_scale = sb.tile([P, O], U8, name="h_scale", align_bytes=64)
         parts = [slice(0, O // 2), slice(O // 2, O)]
-        for half, cols in zip(hid, parts):
+        for cols in parts:
             nc.vector.tensor_tensor(
-                out=half[:].rearrange("p (c i) t -> p c t i", i=4),
+                out=hid[:, cols, :].rearrange("p (c i) t -> p c t i", i=4),
                 in0=from_board[:, :, cols].rearrange("p t (c i) -> p c t i", i=4),
                 in1=from_slot[:, :, cols].rearrange("p t (c i) -> p c t i", i=4),
                 op=MAX,
             )
-        for half, cols in zip(hid, parts):
+        for cols in parts:
             nc.vector.quantize_mx(
                 out=h_code[:, cols].bitcast(E4M3), scales=h_scale[:, cols],
-                in_=half[:].rearrange("p o t -> p (o t)"),
+                in_=hid[:, cols, :].rearrange("p o t -> p (o t)"),
             )
 
         halves = N // P

@@ -55,8 +55,8 @@ def tile_list_leadboard_twow_store_pagetwice_kernel(
         def deal(engine_copy, src, dtype, name, tag=None):
             t = sb.tile([P, R], dtype, name=name, tag=tag or name, align_bytes=64)
             engine_copy(
-                out=t[:].rearrange("p (t m) -> p m t", t=PACK),
-                in_=src[:, 0:R].rearrange("p (m t) -> p m t", t=PACK),
+                out=t[:].rearrange("p (t c i) -> p c t i", t=PACK, i=4),
+                in_=src[:].rearrange("p (c i t) -> p c t i", t=PACK, i=4),
             )
             return t
 
@@ -86,16 +86,16 @@ def tile_list_leadboard_twow_store_pagetwice_kernel(
         boards = {t: zeroed(nc.vector, C, "board%d" % t, "board%d" % t) for t in (1, 0, 3)}
 
         ws_rows = sb.tile([PACK, QUADS, R // 4], I32, name="ws_rows")
-        nc.sync.dma_start(ws_rows[:], w_scales[0].rearrange("(q r) c -> r q c", r=PACK).bitcast(I32))
-        x_all = sb.tile([P, T], U32, name="x_all", align_bytes=64)
-        nc.scalar.dma_start(x_all[:].bitcast(I32), xt_words[0].rearrange("p n t -> p (n t)").bitcast(I32))
+        nc.scalar.dma_start(ws_rows[:], w_scales[0].rearrange("(q r) c -> r q c", r=PACK).bitcast(I32))
         l_tok = load_list(offs, "l_tok")
+        x_all = sb.tile([P, T], U32, name="x_all", align_bytes=64)
+        nc.sync.dma_start(x_all[:].bitcast(I32), xt_words[0].rearrange("p n t -> p (n t)").bitcast(I32))
         load_plane(xs_plane, xt_scales)
         w_raw = sb.tile([P, R], U16, name="w_raw", align_bytes=64)
         nc.sync.dma_start(w_raw[:].bitcast(I32), w_words[0].bitcast(I32))
+        l_board = load_list(offs2, "l_board")
         w2_raw = sb.tile([P, R], U32, name="w2_raw", align_bytes=64)
         nc.sync.dma_start(w2_raw[:].bitcast(I32), w2_words[0].rearrange("p n t -> p (n t)").bitcast(I32))
-        l_board = load_list(offs2, "l_board")
         load_plane(w2s_plane, w2_scales)
         l_slot = load_list(offs4, "l_slot")
         l_pick = load_list(offs3, "l_pick")
@@ -179,10 +179,10 @@ def tile_list_leadboard_twow_store_pagetwice_kernel(
 
         pages = [zeroed(nc.gpsimd, E, "page%d" % i, "a%d" % t) for i, t in enumerate((0, 1, 3, 2))]
 
+        v_code = [gather(v_all, l_store[:, entries[0]], P, U16, "v_code0")]
         v_scale = gather(vs_plane, l_store, N, U8, "v_scale")
-        v_code = gather(v_all, l_store, N, U16, "v_code", "vs_plane")
 
-        hid = sb.tile([P, O, PACK], BF16, name="hid", tag="v_all", align_bytes=64)
+        hid = sb.tile([P, O, PACK], BF16, name="hid", tag="vs_plane", align_bytes=64)
         h_code = sb.tile([P, O], U32, name="h_code", align_bytes=64)
         h_scale = sb.tile([P, O], U8, name="h_scale", align_bytes=64)
         parts = [slice(0, O // 2), slice(O // 2, O)]
@@ -199,13 +199,15 @@ def tile_list_leadboard_twow_store_pagetwice_kernel(
                 in_=hid[:, cols, :].rearrange("p o t -> p (o t)"),
             )
 
+        v_code.append(gather(v_all, l_store[:, entries[1]], P, U16, "v_code1", "vs_plane"))
+
         halves = N // P
         p_acc = []
         for h in range(halves):
             acc = psum.tile([P, O], F32, name="p_acc%d" % h, tag="a_acc%d" % h)
             cols = slice(P * h, P * (h + 1))
             nc.tensor.matmul_mx(
-                out=acc[:], lhsT=v_code[:, cols].bitcast(E2M1), lhsT_scale=v_scale[:, cols],
+                out=acc[:], lhsT=v_code[h][:].bitcast(E2M1), lhsT_scale=v_scale[:, cols],
                 rhs=h_code[:].bitcast(E4M3), rhs_scale=h_scale[:], start=True, stop=True,
             )
             p_acc.append(acc)

from contextlib import ExitStack

import concourse.mybir as mybir

K, T, J, R, C, O, N, S, E = 512, 1024, 256, 512, 512, 128, 256, 1024, 512
FLOPS = 2 * (2 * K * R * J + R * N * O)

F32 = mybir.dt.float32
BF16 = mybir.dt.bfloat16
I32 = mybir.dt.int32
U32 = mybir.dt.uint32
U16 = mybir.dt.uint16
U8 = mybir.dt.uint8
E4M3 = mybir.dt.float8_e4m3fn_x4
E5M2 = mybir.dt.float8_e5m2_x4
E2M1 = mybir.dt.float4_e2m1fn_x4
COPY = mybir.ActivationFunctionType.Copy
ADD = mybir.AluOpType.add
MAX = mybir.AluOpType.max

P = 128
PACK = 4
QUADS = 4
QUAD = 32
SPLIT = 256


def tile_list_leadboard_twow_store_pagetwice_kernel(
    tc, xt_words, xt_scales, w_words, w_scales, w2_words, w2_scales, vs_words, vs_scales,
    offs, offs2, offs3, offs4, offs5, offs6, offs7, out,
):
    nc = tc.nc
    with ExitStack() as ctx:
        lists = ctx.enter_context(tc.tile_pool(name="lists", bufs=1))
        sb = ctx.enter_context(tc.tile_pool(name="sb", bufs=1))
        psum = ctx.enter_context(tc.psum_pool(name="psum", bufs=1))

        def load_list(src, name):
            t = lists.tile(list(src.shape), U16, name=name)
            nc.sync.dma_start(t[:], src)
            return t

        def zero_plane(width, name, tag):
            t = sb.tile([P, width], U8, name=name, tag=tag, align_bytes=64)
            nc.vector.memset(t[:].bitcast(I32), 0)
            return t

        def load_plane(plane, src):
            for q in range(QUADS):
                nc.sync.dma_start(
                    plane[QUAD * q : QUAD * q + PACK, :].bitcast(I32),
                    src[0, PACK * q : PACK * (q + 1), :].bitcast(I32),
                )

        def deal(engine_copy, src, dtype, name, tag=None):
            t = sb.tile([P, R], dtype, name=name, tag=tag or name, align_bytes=64)
            engine_copy(
                out=t[:].rearrange("p (t c i) -> p c t i", t=PACK, i=4),
                in_=src[:].rearrange("p (c i t) -> p c t i", t=PACK, i=4),
            )
            return t

        def deal_slice(engine_copy, src, dtype, t, name):
            dealt = sb.tile([P, P], dtype, name=name, tag=name, align_bytes=64)
            engine_copy(out=dealt[:], in_=src[:].rearrange("p (m t) -> p t m", t=PACK)[:, t, :])
            return dealt

        def deal_scales(plane, t, name):
            return deal_slice(nc.gpsimd.tensor_copy, plane, U8, t, name)

        def gather(window, offsets, width, dtype, name, tag=None):
            t = sb.tile([P, width], dtype, name=name, tag=tag or name, align_bytes=64)
            nc.vector.tensor_copy(out=t[:], in_=window[:].indirect(offsets[:]))
            return t

        xs_plane = zero_plane(T, "xs_plane", "xs_plane")
        ws_plane = zero_plane(R, "ws_plane", "ws_plane")
        w2s_plane = zero_plane(R, "w2s_plane", "w2s_plane")
        vs_plane = zero_plane(S, "vs_plane", "vs_plane")

        def zeroed(engine, width, name, tag):
            t = sb.tile([P, width], F32, name=name, tag=tag, align_bytes=64)
            engine.memset(t[:], 0.0)
            return t

        boards = {t: zeroed(nc.vector, C, "board%d" % t, "board%d" % t) for t in (1, 0, 3)}

        ws_rows = sb.tile([PACK, QUADS, R // 4], I32, name="ws_rows")
        nc.scalar.dma_start(ws_rows[:], w_scales[0].rearrange("(q r) c -> r q c", r=PACK).bitcast(I32))
        l_tok = load_list(offs, "l_tok")
        x_all = sb.tile([P, T], U32, name="x_all", align_bytes=64)
        nc.sync.dma_start(x_all[:].bitcast(I32), xt_words[0].rearrange("p n t -> p (n t)").bitcast(I32))
        load_plane(xs_plane, xt_scales)
        w_raw = sb.tile([P, R], U16, name="w_raw", align_bytes=64)
        nc.sync.dma_start(w_raw[:].bitcast(I32), w_words[0].bitcast(I32))
        l_board = load_list(offs2, "l_board")
        w2_raw = sb.tile([P, R], U32, name="w2_raw", align_bytes=64)
        nc.sync.dma_start(w2_raw[:].bitcast(I32), w2_words[0].rearrange("p n t -> p (n t)").bitcast(I32))
        load_plane(w2s_plane, w2_scales)
        l_slot = load_list(offs4, "l_slot")
        l_pick = load_list(offs3, "l_pick")
        v_all = sb.tile([P, S], U16, name="v_all", tag="v_all", align_bytes=64)
        nc.sync.dma_start(v_all[:].bitcast(I32), vs_words[0].bitcast(I32))
        l_store = load_list(offs5, "l_store")
        load_plane(vs_plane, vs_scales)
        l_pages = [load_list(offs6, "l_page_a"), load_list(offs7, "l_page_b")]

        for q in range(QUADS):
            nc.vector.tensor_copy(
                out=ws_plane[QUAD * q : QUAD * q + PACK, :].bitcast(I32), in_=ws_rows[:, q, :]
            )
        w_scale = {t: deal_scales(ws_plane, t, "w_scale%d" % t) for t in (1, 0, 3, 2)}
        w_code = {t: deal_slice(nc.scalar.copy, w_raw, U16, t, "w_code%d" % t)[:] for t in (1, 0, 3, 2)}
        x_scale = sb.tile([P, J], U8, name="x_scale", align_bytes=64)
        x_code = sb.tile([P, J], U32, name="x_code", align_bytes=64)
        slots = [slice(0, J // 2), slice(J // 2, J)]
        entries = [slice(0, J // 32), slice(J // 32, J // 16)]
        for cols, ents in zip(slots, entries):
            nc.vector.tensor_copy(out=x_scale[:, cols], in_=xs_plane[:].indirect(l_tok[:, ents]))
            nc.vector.tensor_copy(out=x_code[:, cols], in_=x_all[:].indirect(l_tok[:, ents]))
        w2_dealt = deal(nc.vector.tensor_copy, w2_raw, U32, "w2_code")
        w2_code = [w2_dealt[:, P * t : P * (t + 1)] for t in range(PACK)]

        def stage_one(code, scale, fmt, t, tag, cols=slice(0, J)):
            acc = psum.tile([P, cols.stop - cols.start], F32, name="acc", tag=tag)
            nc.tensor.matmul_mx(
                out=acc[:], lhsT=code[t].bitcast(fmt), lhsT_scale=scale[t][:],
                rhs=x_code[:, cols].bitcast(E5M2), rhs_scale=x_scale[:, cols], start=True, stop=True,
            )
            return acc

        def to_sbuf(engine_copy, acc, width, name):
            t = sb.tile([P, width], F32, name=name, tag=name, align_bytes=64)
            engine_copy(out=t[:], in_=acc[:])
            return t

        def scatter_vector(window, offsets, values):
            nc.vector.tensor_copy(out=window[:].indirect(offsets[:]), in_=values[:])

        def scatter_scalar(window, offsets, values):
            nc.scalar.activation(out=window[:].indirect(offsets[:]), in_=values[:], func=COPY)

        a = [sb.tile([P, J], F32, name="a%d" % t, tag="a%d" % t, align_bytes=64) for t in range(PACK)]
        lo, hi = slots
        acc = stage_one(w_code, w_scale, E2M1, 1, "a_acc1", lo)
        nc.scalar.copy(out=a[1][:, lo], in_=acc[:])
        nc.scalar.activation(
            out=boards[1][:].indirect(l_board[:, entries[0]]), in_=a[1][:, lo], func=COPY
        )
        acc = stage_one(w_code, w_scale, E2M1, 0, "a_acc0")
        nc.vector.tensor_copy(out=a[0][:], in_=acc[:])
        acc = stage_one(w_code, w_scale, E2M1, 1, "a_acc1", hi)
        nc.vector.tensor_copy(out=a[1][:, hi], in_=acc[:])
        acc = stage_one(w_code, w_scale, E2M1, 3, "a_acc3")
        nc.vector.tensor_copy(out=a[3][:], in_=acc[:])
        nc.scalar.activation(
            out=boards[1][:].indirect(l_board[:, entries[1]]), in_=a[1][:, hi], func=COPY
        )
        scatter_vector(boards[0], l_board, a[0])
        acc = stage_one(w_code, w_scale, E2M1, 2, "a_acc2")
        nc.scalar.copy(out=a[2][:], in_=acc[:])
        scatter_scalar(boards[3], l_board, a[3])
        w2_scale = [deal_scales(w2s_plane, t, "w2_scale%d" % t) for t in range(PACK)]
        b_acc = [stage_one(w2_code, w2_scale, E4M3, t, "b_acc%d" % t) for t in range(PACK)]
        b = [to_sbuf(nc.vector.tensor_copy, b_acc[t], J, "b%d" % t) for t in range(PACK)]
        boards[2] = zeroed(nc.gpsimd, C, "board2", "w2_scale3")
        scatter_vector(boards[2], l_board, a[2])

        from_board = sb.tile([P, PACK, O], F32, name="from_board")
        from_slot = sb.tile([P, PACK, O], F32, name="from_slot")
        for t in range(PACK):
            nc.scalar.activation(
                out=from_slot[:, t, :], in_=b[t][:].indirect(l_slot[:]), func=COPY, scale=a[t][:, 0:1]
            )
        for t in (0, 1, 3, 2):
            nc.scalar.activation(
                out=from_board[:, t, :], in_=boards[t][:].indirect(l_pick[:]), func=COPY, scale=b[t][:, 0:1]
            )

        pages = [zeroed(nc.gpsimd, E, "page%d" % i, "a%d" % t) for i, t in enumerate((0, 1, 3, 2))]

        v_code = [gather(v_all, l_store[:, entries[0]], P, U16, "v_code0")]
        v_scale = gather(vs_plane, l_store, N, U8, "v_scale")

        hid = sb.tile([P, O, PACK], BF16, name="hid", tag="vs_plane", align_bytes=64)
        h_code = sb.tile([P, O], U32, name="h_code", align_bytes=64)
        h_scale = sb.tile([P, O], U8, name="h_scale", align_bytes=64)
        parts = [slice(0, O // 2), slice(O // 2, O)]
        for cols in parts:
            nc.vector.tensor_tensor(
                out=hid[:, cols, :].rearrange("p (c i) t -> p c t i", i=4),
                in0=from_board[:, :, cols].rearrange("p t (c i) -> p c t i", i=4),
                in1=from_slot[:, :, cols].rearrange("p t (c i) -> p c t i", i=4),
                op=MAX,
            )
        for cols in parts:
            nc.vector.quantize_mx(
                out=h_code[:, cols].bitcast(E4M3), scales=h_scale[:, cols],
                in_=hid[:, cols, :].rearrange("p o t -> p (o t)"),
            )

        v_code.append(gather(v_all, l_store[:, entries[1]], P, U16, "v_code1", "vs_plane"))

        halves = N // P
        p_acc = []
        for h in range(halves):
            acc = psum.tile([P, O], F32, name="p_acc%d" % h, tag="a_acc%d" % h)
            cols = slice(P * h, P * (h + 1))
            nc.tensor.matmul_mx(
                out=acc[:], lhsT=v_code[h][:].bitcast(E2M1), lhsT_scale=v_scale[:, cols],
                rhs=h_code[:].bitcast(E4M3), rhs_scale=h_scale[:], start=True, stop=True,
            )
            p_acc.append(acc)
        p = [
            to_sbuf(nc.vector.tensor_copy, p_acc[0], O, "p0"),
            to_sbuf(nc.scalar.copy, p_acc[1], O, "p1"),
        ]
        for h in range(halves):
            scatter_vector(pages[2 * h], l_pages[0], p[h])
            scatter_scalar(pages[2 * h + 1], l_pages[1], p[h])

        def add_pages(engine, y, h, cols):
            engine.tensor_tensor(
                out=y[:, cols], in0=pages[2 * h][:, cols], in1=pages[2 * h + 1][:, cols], op=ADD
            )

        y0 = sb.tile([P, E], F32, name="y0")
        add_pages(nc.gpsimd, y0, 0, slice(0, SPLIT))
        nc.sync.dma_start(out[0:P, 0:SPLIT], y0[:, 0:SPLIT])
        add_pages(nc.vector, y0, 0, slice(SPLIT, E))
        nc.sync.dma_start(out[0:P, SPLIT:E], y0[:, SPLIT:E])
        y1 = sb.tile([P, E], F32, name="y1")
        for cols in (slice(0, E // 2), slice(E // 2, E)):
            add_pages(nc.vector, y1, 1, cols)
            nc.sync.dma_start(out[P : 2 * P, cols], y1[:, cols])
